import numpy as np, ml_dtypes
CORES = [3,5,19,21,35,37,51,53,67,69]
N = 10
R, T = 4096, 512
def entries(a): return a.T.reshape(-1)
def pack(v, P): return np.ascontiguousarray(np.asarray(v, np.int32).reshape(-1, P).T)
def lists(rng, how):
    I = rng.integers(0, N * R, (N, T))
    if how == "alike": I[:] = rng.integers(0, N * R, (N, 1))
    if how == "distinct": I = np.stack([rng.permutation(N * R)[:T] for r in range(N)])
    if how == "hotrank": I = R * int(rng.integers(N)) + rng.integers(0, R, (N, T))
    if how == "own": I = R * np.arange(N).reshape(N, 1) + rng.integers(0, R, (N, T))
    if how == "edge": I = R * rng.integers(0, N, (N, T)) + np.where(rng.random((N, T)) < 0.5, 0, R - 1)
    return {"idx": np.stack([pack(I[r], 16) for r in range(N)])}
def setup_inputs(rng):
    return dict({"tab": rng.standard_normal((N, 128, R), dtype=np.float32).astype(ml_dtypes.bfloat16)}, **lists(rng, "uniform"))
def setup_inputs_alike(rng):
    d = setup_inputs(rng); d.update(lists(rng, "alike"))
    for k in ("tab",): d[k] = (d[k].astype(np.float32) * 1048576.0).astype(d[k].dtype)
    return d
def setup_inputs_distinct(rng):
    d = setup_inputs(rng); d.update(lists(rng, "distinct"))
    for k in ("tab",): d[k] = (d[k].astype(np.float32) * (1 / 1024.0)).astype(d[k].dtype)
    return d
def setup_inputs_edge(rng):
    d = setup_inputs(rng); d.update(lists(rng, "edge"))
    return d
def setup_inputs_hotrank(rng):
    d = setup_inputs(rng); d.update(lists(rng, "hotrank"))
    return d
def setup_inputs_own(rng):
    d = setup_inputs(rng); d.update(lists(rng, "own"))
    return d
def check_inputs(x):
    bad = []
    if x["idx"].min() < 0 or x["idx"].max() >= N * R: bad.append("idx out of range")
    return bad
def reference(tab, idx):
    A = np.concatenate(list(tab), axis=1)
    return {"y": np.stack([A[:, entries(idx[r])] for r in range(N)])}

@@ -1,0 +1,156 @@
+import comms_topo
+from concourse.bass import DstId, RemoteDMATransfer
+from concourse.mybir import AluOpType, ActivationFunctionType
+
+CORES = [3, 5, 19, 21, 35, 37, 51, 53, 67, 69]
+N, R, TT = 10, 4096, 512
+CHIPS = sorted({comms_topo.chip(c) for c in CORES})
+NCH = len(CHIPS)
+G = N // NCH
+W = G * R
+SHIFT = W.bit_length() - 1
+LC = TT // 16
+KP = 16 * NCH
+BLOCKS = [(0, R // 2), (R // 2, R)]
+
+SCRATCH = {
+    "win": ("sbuf", [128, W], "bfloat16"),
+    "lst": ("dram", [128 * NCH, 4], "int32"),
+    "ls": ("sbuf", [128, LC], "int32"),
+    "lm": ("sbuf", [128, LC], "int32"),
+    "lmf": ("sbuf", [128, LC], "float32"),
+    "lh": ("sbuf", [128, LC], "int32"),
+    "lhf": ("sbuf", [128, LC], "float32"),
+    "jk": ("sbuf", [128, LC], "float32"),
+    "iv": ("sbuf", [128, 128 * NCH], "int32"),
+    "sel": ("sbuf", [128, 128 * NCH], "float32"),
+    "po": ("psum", [128, 512], "float32"),
+    "pf": ("psum", [128, 512], "float32"),
+    "off": ("sbuf", [128, LC * NCH], "uint16"),
+    "fo": ("sbuf", [128, LC], "uint16"),
+    "resp": ("sbuf", [128, TT * (NCH - 1)], "bfloat16"),
+    "land": ("sbuf", [128, TT * NCH], "bfloat16"),
+    "yo": ("sbuf", [128, TT], "bfloat16"),
+}
+SEMAPHORES = (["idx", "lists", "ls", "x", "loc", "iv", "jk", "sel", "lm", "lmf", "lh", "lhf", "mm", "mmf", "off", "fo",
+               "own", "arr", "y", "st"]
+              + ["ld%d" % b for b in range(len(BLOCKS))] + ["g%d" % i for i in range(NCH - 1)])
+
+
+def _bits(m):
+    return bin(m).count("1")
+
+
+def rank_program(g, core, T, topo):
+    rank = T.rank_of(core)
+    if rank is None:
+        return
+    S = T.sem
+    cores = list(T.cores)
+    k = CHIPS.index(topo.chip(core))
+    here = [r for r in range(N) if topo.chip(cores[r]) == topo.chip(core)]
+    assert here == list(range(G * k, G * k + G))
+    others = [cores[r] for r in here if r != rank]
+    peer = {}
+    for c in cores:
+        if topo.die(c) == topo.die(core) and c != core:
+            peer[CHIPS.index(topo.chip(c))] = c
+    assert sorted(peer) == [s for s in range(NCH) if s != k]
+    order = [(k + 1 + i) % NCH for i in range(NCH - 1)]
+    base = R * here.index(rank)
+    v, sc, sy, te = g.vector, g.scalar, g.sync, g.tensor
+    mine = T.lst[128 * k:128 * k + 128, :]
+
+    sy.dma_start(mine, T.idx[:]).then_inc(S.idx, 16)
+    for b, (c0, c1) in enumerate(BLOCKS):
+        sy.dma_start(T.win[:, base + c0:base + c1], T.tab[:, c0:c1]).then_inc(S["ld%d" % b], 16)
+
+    g.iota(T.iv[0:KP, :], [[-16, NCH], [0, 8], [-1, 16]], 0, 1).then_inc(S.iv, 1)
+    g.iota(T.jk[0:KP, :], [[16, LC]], -16 * k, 1, allow_small_or_imprecise_dtypes=True).then_inc(S.jk, 1)
+
+    sent = 0
+    lmask = topo.mask(core, peer[order[0]])
+    for s in order:
+        assert topo.may_write(core, peer[s]) and topo.mask(core, peer[s]) == lmask
+    g.wait_ge(S.idx, 16)
+    g.remote_dma_fused([RemoteDMATransfer(
+        dst_ids=[DstId(rid=topo.addr(peer[s])[0], pnc=topo.addr(peer[s])[1]) for s in order],
+        dma_engine_mask=lmask, remote_sem=S.lists, srcs=[mine], dsts=[mine for s in order], alu_op=0)], local_sem=S.loc)
+    sent += _bits(lmask)
+
+    xin = 0
+    for b, (c0, c1) in enumerate(BLOCKS):
+        g.wait_ge(S["ld%d" % b], 16)
+        for o in others:
+            rid, pid, _ = topo.addr(o)
+            m = topo.mask(core, o)
+            blk = T.win[:, base + c0:base + c1]
+            g.remote_dma(blk, blk, S.x, S.loc, pid, rid, m)
+            sent += _bits(m)
+            xin += _bits(topo.mask(o, core))
+
+    sy.wait_ge(S.idx, 16)
+    sy.wait_ge(S.lists, (NCH - 1) * _bits(lmask))
+    sy.dma_start(T.ls[0:KP, :], T.lst[:, :]).then_inc(S.ls, 16)
+
+    v.wait_ge(S.iv, 1)
+    v.tensor_scalar(T.sel[0:KP, :], T.iv[0:KP, :], 0, None, AluOpType.is_equal).then_inc(S.sel, 1)
+    v.wait_ge(S.ls, 16)
+    v.tensor_scalar(T.lm[0:KP, :], T.ls[0:KP, :], W - 1, None, AluOpType.bitwise_and).then_inc(S.lm, 1)
+    v.wait_ge(S.lm, 1)
+    v.tensor_copy(T.lmf[0:KP, :], T.lm[0:KP, :]).then_inc(S.lmf, 1)
+    v.tensor_scalar(T.lh[0:KP, :], T.ls[0:KP, :], SHIFT - 9, 0xFFFF ^ (TT - 1), AluOpType.logical_shift_right,
+                    AluOpType.bitwise_and).then_inc(S.lh, 1)
+    v.wait_ge(S.lh, 1)
+    v.tensor_copy(T.lhf[0:KP, :], T.lh[0:KP, :]).then_inc(S.lhf, 1)
+
+    te.wait_ge(S.sel, 1)
+    te.wait_ge(S.lmf, 1)
+    for s in order + [k]:
+        te.matmul(T.po[:, LC * s:LC * s + LC], T.sel[0:KP, 128 * s:128 * s + 128], T.lmf[0:KP, :], True, True).then_inc(S.mm, 1)
+    te.wait_ge(S.lhf, 1)
+    te.wait_ge(S.jk, 1)
+    te.matmul(T.pf[:, 0:LC], T.sel[0:KP, 128 * k:128 * k + 128], T.lhf[0:KP, :], True, False)
+    te.matmul(T.pf[:, 0:LC], T.sel[0:KP, 128 * k:128 * k + 128], T.jk[0:KP, :], False, True).then_inc(S.mmf, 1)
+
+    v.wait_ge(S.mm, NCH)
+    v.tensor_copy(T.off[:, :], T.po[:, 0:LC * NCH]).then_inc(S.off, 1)
+
+    def src(s):
+        return T.win[:, 0:W].indirect(T.off[:, LC * s:LC * s + LC])
+
+    for q in (v, sc):
+        q.wait_ge(S.off, 1)
+        for b in range(len(BLOCKS)):
+            q.wait_ge(S["ld%d" % b], 16)
+        q.wait_ge(S.x, xin)
+    for i, s in enumerate(order):
+        out = T.resp[:, TT * i:TT * i + TT]
+        if i % 2 == 0:
+            v.tensor_copy(out, src(s)).then_inc(S["g%d" % i], 1)
+        else:
+            sc.activation(out, src(s), ActivationFunctionType.Copy).then_inc(S["g%d" % i], 1)
+    v.tensor_copy(T.land[:, TT * k:TT * k + TT], src(k)).then_inc(S.own, 1)
+    v.wait_ge(S.mmf, 1)
+    v.tensor_copy(T.fo[:, :], T.pf[:, 0:LC]).then_inc(S.fo, 1)
+
+    for i, s in enumerate(order):
+        rid, pid, _ = topo.addr(peer[s])
+        m = topo.mask(core, peer[s])
+        g.wait_ge(S["g%d" % i], 1)
+        g.remote_dma(T.land[:, TT * k:TT * k + TT], T.resp[:, TT * i:TT * i + TT], S.arr, S.loc, pid, rid, m)
+        sent += _bits(m)
+    arrive = sum(_bits(topo.mask(peer[s], core)) for s in order)
+
+    h = LC // 2
+    for q in (v, sc):
+        q.wait_ge(S.fo, 1)
+        q.wait_ge(S.own, 1)
+        q.wait_ge(S.arr, arrive)
+    v.tensor_copy(T.yo[:, 0:16 * h], T.land[:, :].indirect(T.fo[:, 0:h])).then_inc(S.y, 1)
+    sc.activation(T.yo[:, 16 * h:TT], T.land[:, :].indirect(T.fo[:, h:LC]), ActivationFunctionType.Copy).then_inc(S.y, 1)
+    sy.wait_ge(S.y, 2)
+    sy.dma_start(T.y[:, :], T.yo[:, :]).then_inc(S.st, 16)
+
+    g.wait_ge(S.loc, sent)
+    g.wait_ge(S.st, 16)

@@ -17,14 +17,12 @@ SCRATCH = {
     "win": ("sbuf", [128, W], "bfloat16"),
     "lst": ("dram", [128 * NCH, 4], "int32"),
     "ls": ("sbuf", [128, LC], "int32"),
-    "lm": ("sbuf", [128, LC], "int32"),
     "lmf": ("sbuf", [128, LC], "float32"),
     "lh": ("sbuf", [128, LC], "int32"),
     "lhf": ("sbuf", [128, LC], "float32"),
     "jk": ("sbuf", [128, LC], "float32"),
     "iv": ("sbuf", [128, 128 * NCH], "int32"),
     "sel": ("sbuf", [128, 128 * NCH], "float32"),
-    "po": ("psum", [128, 512], "float32"),
     "pf": ("psum", [128, 512], "float32"),
     "off": ("sbuf", [128, LC * NCH], "uint16"),
     "fo": ("sbuf", [128, LC], "uint16"),
@@ -32,9 +30,11 @@ SCRATCH = {
     "land": ("sbuf", [128, TT * NCH], "bfloat16"),
     "yo": ("sbuf", [128, TT], "bfloat16"),
 }
-SEMAPHORES = (["idx", "lists", "ls", "x", "loc", "iv", "jk", "sel", "lm", "lmf", "lh", "lhf", "mm", "mmf", "off", "fo",
-               "own", "arr", "y", "st"]
-              + ["ld%d" % b for b in range(len(BLOCKS))] + ["g%d" % i for i in range(NCH - 1)])
+for _i in range(NCH):
+    SCRATCH["po%d" % _i] = ("psum", [128, 512], "float32")
+SEMAPHORES = (["idx", "lists", "ls", "x", "loc", "iv", "jk", "sel", "lmf", "lh", "lhf", "mmf", "fo", "arr", "y", "st"]
+              + ["ld%d" % b for b in range(len(BLOCKS))]
+              + [n + str(i) for i in range(NCH) for n in ("mm", "o", "g")])
 
 
 def _bits(m):
@@ -93,59 +93,70 @@ def rank_program(g, core, T, topo):
     sy.wait_ge(S.lists, (NCH - 1) * _bits(lmask))
     sy.dma_start(T.ls[0:KP, :], T.lst[:, :]).then_inc(S.ls, 16)
 
+    serve = order + [k]
     v.wait_ge(S.iv, 1)
     v.tensor_scalar(T.sel[0:KP, :], T.iv[0:KP, :], 0, None, AluOpType.is_equal).then_inc(S.sel, 1)
     v.wait_ge(S.ls, 16)
-    v.tensor_scalar(T.lm[0:KP, :], T.ls[0:KP, :], W - 1, None, AluOpType.bitwise_and).then_inc(S.lm, 1)
-    v.wait_ge(S.lm, 1)
-    v.tensor_copy(T.lmf[0:KP, :], T.lm[0:KP, :]).then_inc(S.lmf, 1)
+    v.tensor_scalar(T.lmf[0:KP, :], T.ls[0:KP, :], -W * k, None, AluOpType.add).then_inc(S.lmf, 1)
+    te.wait_ge(S.sel, 1)
+    te.wait_ge(S.lmf, 1)
+    for i, s in enumerate(serve):
+        te.matmul(T["po%d" % i][:, 0:LC], T.sel[0:KP, 128 * s:128 * s + 128], T.lmf[0:KP, :], True,
+                  True).then_inc(S["mm%d" % i], 1)
+
+    h = LC // 2
+
+    def clamp(i):
+        v.wait_ge(S["mm%d" % i], 1)
+        v.tensor_scalar(T.off[:, LC * i:LC * i + LC], T["po%d" % i][:, 0:LC], 0, W - 1, AluOpType.max,
+                        AluOpType.min).then_inc(S["o%d" % i], 1)
+
+    def answer(i, q):
+        buf, c = (T.resp, TT * i) if i < NCH - 1 else (T.land, TT * k)
+        q.wait_ge(S["o%d" % i], 1)
+        if q is v:
+            v.tensor_copy(buf[:, c:c + 16 * h],
+                          T.win[:, 0:W].indirect(T.off[:, LC * i:LC * i + h])).then_inc(S["g%d" % i], 1)
+        else:
+            sc.activation(buf[:, c + 16 * h:c + TT], T.win[:, 0:W].indirect(T.off[:, LC * i + h:LC * i + LC]),
+                          ActivationFunctionType.Copy).then_inc(S["g%d" % i], 1)
+
+    clamp(0)
+    for q in (v, sc):
+        for b in range(len(BLOCKS)):
+            q.wait_ge(S["ld%d" % b], 16)
+        q.wait_ge(S.x, xin)
+    done = 1
+    for i in range(NCH):
+        answer(i, v)
+        answer(i, sc)
+        for n in range(2):
+            if done < NCH:
+                clamp(done)
+                done += 1
+
     v.tensor_scalar(T.lh[0:KP, :], T.ls[0:KP, :], SHIFT - 9, 0xFFFF ^ (TT - 1), AluOpType.logical_shift_right,
                     AluOpType.bitwise_and).then_inc(S.lh, 1)
     v.wait_ge(S.lh, 1)
     v.tensor_copy(T.lhf[0:KP, :], T.lh[0:KP, :]).then_inc(S.lhf, 1)
-
-    te.wait_ge(S.sel, 1)
-    te.wait_ge(S.lmf, 1)
-    for s in order + [k]:
-        te.matmul(T.po[:, LC * s:LC * s + LC], T.sel[0:KP, 128 * s:128 * s + 128], T.lmf[0:KP, :], True, True).then_inc(S.mm, 1)
     te.wait_ge(S.lhf, 1)
     te.wait_ge(S.jk, 1)
     te.matmul(T.pf[:, 0:LC], T.sel[0:KP, 128 * k:128 * k + 128], T.lhf[0:KP, :], True, False)
     te.matmul(T.pf[:, 0:LC], T.sel[0:KP, 128 * k:128 * k + 128], T.jk[0:KP, :], False, True).then_inc(S.mmf, 1)
-
-    v.wait_ge(S.mm, NCH)
-    v.tensor_copy(T.off[:, :], T.po[:, 0:LC * NCH]).then_inc(S.off, 1)
-
-    def src(s):
-        return T.win[:, 0:W].indirect(T.off[:, LC * s:LC * s + LC])
-
-    for q in (v, sc):
-        q.wait_ge(S.off, 1)
-        for b in range(len(BLOCKS)):
-            q.wait_ge(S["ld%d" % b], 16)
-        q.wait_ge(S.x, xin)
-    for i, s in enumerate(order):
-        out = T.resp[:, TT * i:TT * i + TT]
-        if i % 2 == 0:
-            v.tensor_copy(out, src(s)).then_inc(S["g%d" % i], 1)
-        else:
-            sc.activation(out, src(s), ActivationFunctionType.Copy).then_inc(S["g%d" % i], 1)
-    v.tensor_copy(T.land[:, TT * k:TT * k + TT], src(k)).then_inc(S.own, 1)
     v.wait_ge(S.mmf, 1)
     v.tensor_copy(T.fo[:, :], T.pf[:, 0:LC]).then_inc(S.fo, 1)
 
     for i, s in enumerate(order):
         rid, pid, _ = topo.addr(peer[s])
         m = topo.mask(core, peer[s])
-        g.wait_ge(S["g%d" % i], 1)
+        g.wait_ge(S["g%d" % i], 2)
         g.remote_dma(T.land[:, TT * k:TT * k + TT], T.resp[:, TT * i:TT * i + TT], S.arr, S.loc, pid, rid, m)
         sent += _bits(m)
     arrive = sum(_bits(topo.mask(peer[s], core)) for s in order)
 
-    h = LC // 2
     for q in (v, sc):
         q.wait_ge(S.fo, 1)
-        q.wait_ge(S.own, 1)
+        q.wait_ge(S["g%d" % (NCH - 1)], 2)
         q.wait_ge(S.arr, arrive)
     v.tensor_copy(T.yo[:, 0:16 * h], T.land[:, :].indirect(T.fo[:, 0:h])).then_inc(S.y, 1)
     sc.activation(T.yo[:, 16 * h:TT], T.land[:, :].indirect(T.fo[:, h:LC]), ActivationFunctionType.Copy).then_inc(S.y, 1)

import comms_topo
from concourse.bass import DstId, RemoteDMATransfer
from concourse.mybir import AluOpType, ActivationFunctionType

CORES = [3, 5, 19, 21, 35, 37, 51, 53, 67, 69]
N, R, TT = 10, 4096, 512
CHIPS = sorted({comms_topo.chip(c) for c in CORES})
NCH = len(CHIPS)
G = N // NCH
W = G * R
SHIFT = W.bit_length() - 1
LC = TT // 16
KP = 16 * NCH
BLOCKS = [(0, R // 2), (R // 2, R)]

SCRATCH = {
    "win": ("sbuf", [128, W], "bfloat16"),
    "lst": ("dram", [128 * NCH, 4], "int32"),
    "ls": ("sbuf", [128, LC], "int32"),
    "lmf": ("sbuf", [128, LC], "float32"),
    "lh": ("sbuf", [128, LC], "int32"),
    "lhf": ("sbuf", [128, LC], "float32"),
    "jk": ("sbuf", [128, LC], "float32"),
    "iv": ("sbuf", [128, 128 * NCH], "int32"),
    "sel": ("sbuf", [128, 128 * NCH], "float32"),
    "pf": ("psum", [128, 512], "float32"),
    "off": ("sbuf", [128, LC * NCH], "uint16"),
    "fo": ("sbuf", [128, LC], "uint16"),
    "resp": ("sbuf", [128, TT * (NCH - 1)], "bfloat16"),
    "land": ("sbuf", [128, TT * NCH], "bfloat16"),
    "yo": ("sbuf", [128, TT], "bfloat16"),
}
for _i in range(NCH):
    SCRATCH["po%d" % _i] = ("psum", [128, 512], "float32")
SEMAPHORES = (["idx", "lists", "ls", "x", "loc", "iv", "jk", "sel", "lmf", "lh", "lhf", "mmf", "fo", "arr", "y", "st"]
              + ["ld%d" % b for b in range(len(BLOCKS))]
              + [n + str(i) for i in range(NCH) for n in ("mm", "o", "g")])


def _bits(m):
    return bin(m).count("1")


def rank_program(g, core, T, topo):
    rank = T.rank_of(core)
    if rank is None:
        return
    S = T.sem
    cores = list(T.cores)
    k = CHIPS.index(topo.chip(core))
    here = [r for r in range(N) if topo.chip(cores[r]) == topo.chip(core)]
    assert here == list(range(G * k, G * k + G))
    others = [cores[r] for r in here if r != rank]
    peer = {}
    for c in cores:
        if topo.die(c) == topo.die(core) and c != core:
            peer[CHIPS.index(topo.chip(c))] = c
    assert sorted(peer) == [s for s in range(NCH) if s != k]
    order = [(k + 1 + i) % NCH for i in range(NCH - 1)]
    base = R * here.index(rank)
    v, sc, sy, te = g.vector, g.scalar, g.sync, g.tensor
    mine = T.lst[128 * k:128 * k + 128, :]

    sy.dma_start(mine, T.idx[:]).then_inc(S.idx, 16)
    for b, (c0, c1) in enumerate(BLOCKS):
        sy.dma_start(T.win[:, base + c0:base + c1], T.tab[:, c0:c1]).then_inc(S["ld%d" % b], 16)

    g.iota(T.iv[0:KP, :], [[-16, NCH], [0, 8], [-1, 16]], 0, 1).then_inc(S.iv, 1)
    g.iota(T.jk[0:KP, :], [[16, LC]], -16 * k, 1, allow_small_or_imprecise_dtypes=True).then_inc(S.jk, 1)

    sent = 0
    lmask = topo.mask(core, peer[order[0]])
    for s in order:
        assert topo.may_write(core, peer[s]) and topo.mask(core, peer[s]) == lmask
    g.wait_ge(S.idx, 16)
    g.remote_dma_fused([RemoteDMATransfer(
        dst_ids=[DstId(rid=topo.addr(peer[s])[0], pnc=topo.addr(peer[s])[1]) for s in order],
        dma_engine_mask=lmask, remote_sem=S.lists, srcs=[mine], dsts=[mine for s in order], alu_op=0)], local_sem=S.loc)
    sent += _bits(lmask)

    xin = 0
    for b, (c0, c1) in enumerate(BLOCKS):
        g.wait_ge(S["ld%d" % b], 16)
        for o in others:
            rid, pid, _ = topo.addr(o)
            m = topo.mask(core, o)
            blk = T.win[:, base + c0:base + c1]
            g.remote_dma(blk, blk, S.x, S.loc, pid, rid, m)
            sent += _bits(m)
            xin += _bits(topo.mask(o, core))

    sy.wait_ge(S.idx, 16)
    sy.wait_ge(S.lists, (NCH - 1) * _bits(lmask))
    sy.dma_start(T.ls[0:KP, :], T.lst[:, :]).then_inc(S.ls, 16)

    serve = order + [k]
    v.wait_ge(S.iv, 1)
    v.tensor_scalar(T.sel[0:KP, :], T.iv[0:KP, :], 0, None, AluOpType.is_equal).then_inc(S.sel, 1)
    v.wait_ge(S.ls, 16)
    v.tensor_scalar(T.lmf[0:KP, :], T.ls[0:KP, :], -W * k, None, AluOpType.add).then_inc(S.lmf, 1)
    te.wait_ge(S.sel, 1)
    te.wait_ge(S.lmf, 1)
    for i, s in enumerate(serve):
        te.matmul(T["po%d" % i][:, 0:LC], T.sel[0:KP, 128 * s:128 * s + 128], T.lmf[0:KP, :], True,
                  True).then_inc(S["mm%d" % i], 1)

    h = LC // 2

    def clamp(i):
        v.wait_ge(S["mm%d" % i], 1)
        v.tensor_scalar(T.off[:, LC * i:LC * i + LC], T["po%d" % i][:, 0:LC], 0, W - 1, AluOpType.max,
                        AluOpType.min).then_inc(S["o%d" % i], 1)

    def answer(i, q):
        buf, c = (T.resp, TT * i) if i < NCH - 1 else (T.land, TT * k)
        q.wait_ge(S["o%d" % i], 1)
        if q is v:
            v.tensor_copy(buf[:, c:c + 16 * h],
                          T.win[:, 0:W].indirect(T.off[:, LC * i:LC * i + h])).then_inc(S["g%d" % i], 1)
        else:
            sc.activation(buf[:, c + 16 * h:c + TT], T.win[:, 0:W].indirect(T.off[:, LC * i + h:LC * i + LC]),
                          ActivationFunctionType.Copy).then_inc(S["g%d" % i], 1)

    clamp(0)
    for q in (v, sc):
        for b in range(len(BLOCKS)):
            q.wait_ge(S["ld%d" % b], 16)
        q.wait_ge(S.x, xin)
    done = 1
    for i in range(NCH):
        answer(i, v)
        answer(i, sc)
        for n in range(2):
            if done < NCH:
                clamp(done)
                done += 1

    v.tensor_scalar(T.lh[0:KP, :], T.ls[0:KP, :], SHIFT - 9, 0xFFFF ^ (TT - 1), AluOpType.logical_shift_right,
                    AluOpType.bitwise_and).then_inc(S.lh, 1)
    v.wait_ge(S.lh, 1)
    v.tensor_copy(T.lhf[0:KP, :], T.lh[0:KP, :]).then_inc(S.lhf, 1)
    te.wait_ge(S.lhf, 1)
    te.wait_ge(S.jk, 1)
    te.matmul(T.pf[:, 0:LC], T.sel[0:KP, 128 * k:128 * k + 128], T.lhf[0:KP, :], True, False)
    te.matmul(T.pf[:, 0:LC], T.sel[0:KP, 128 * k:128 * k + 128], T.jk[0:KP, :], False, True).then_inc(S.mmf, 1)
    v.wait_ge(S.mmf, 1)
    v.tensor_copy(T.fo[:, :], T.pf[:, 0:LC]).then_inc(S.fo, 1)

    for i, s in enumerate(order):
        rid, pid, _ = topo.addr(peer[s])
        m = topo.mask(core, peer[s])
        g.wait_ge(S["g%d" % i], 2)
        g.remote_dma(T.land[:, TT * k:TT * k + TT], T.resp[:, TT * i:TT * i + TT], S.arr, S.loc, pid, rid, m)
        sent += _bits(m)
    arrive = sum(_bits(topo.mask(peer[s], core)) for s in order)

    for q in (v, sc):
        q.wait_ge(S.fo, 1)
        q.wait_ge(S["g%d" % (NCH - 1)], 2)
        q.wait_ge(S.arr, arrive)
    v.tensor_copy(T.yo[:, 0:16 * h], T.land[:, :].indirect(T.fo[:, 0:h])).then_inc(S.y, 1)
    sc.activation(T.yo[:, 16 * h:TT], T.land[:, :].indirect(T.fo[:, h:LC]), ActivationFunctionType.Copy).then_inc(S.y, 1)
    sy.wait_ge(S.y, 2)
    sy.dma_start(T.y[:, :], T.yo[:, :]).then_inc(S.st, 16)

    g.wait_ge(S.loc, sent)
    g.wait_ge(S.st, 16)
